import numpy as np
import ml_dtypes

BF16 = ml_dtypes.bfloat16


def bf(x):
    return np.asarray(x, np.float32).astype(BF16)


def f32(x):
    return np.asarray(x, np.float32)


def f64(x):
    return np.asarray(x).astype(np.float64)


def striped(idx):
    return np.tile(idx.reshape(-1, 16).T, (8, 1))


S, K, M, N, E, Q = 256, 128, 128, 512, 4, 128


def two_experts():
    first = np.random.permutation(S).reshape(E, S // E)
    return np.concatenate([np.random.permutation(np.concatenate([first[e], first[(e + 1) % E]])) for e in range(E)])


def setup_inputs():
    return {"table": bf(np.random.standard_normal((K, S))), "w": bf(np.random.standard_normal((E, K, M)) / np.sqrt(K)), "c": f32(0.2 + 0.8 * np.random.random_sample((1, N))), "offs": striped(two_experts())}


def reference(table, w, c, offs):
    idx = offs[:16].T.reshape(-1)
    x = f64(table)[:, idx]
    y = np.concatenate([f64(w)[e].T @ x[:, e * Q : (e + 1) * Q] for e in range(E)], axis=1)
    return y * f64(c)

@@ -1,0 +1,39 @@
+import concourse.mybir as mybir
+
+BF16, F32, U16 = mybir.dt.bfloat16, mybir.dt.float32, mybir.dt.uint16
+
+P = 128
+TOKENS = 256
+EXPERTS = 4
+PIECE = 128
+ENTRIES = EXPERTS * PIECE
+PIECE_COLUMNS = PIECE // 16
+
+FLOPS = 2 * P * P * ENTRIES
+
+
+def tile_gather_matmul_kernel(tc, table, w, c, offs, out):
+    nc = tc.nc
+    with (
+        tc.tile_pool(name="held", bufs=1) as held,
+        tc.psum_pool(name="banks", bufs=EXPERTS) as banks,
+    ):
+        gains = held.tile([P, ENTRIES], F32, name="gains")
+        nc.scalar.dma_start(gains[:], c.rearrange("o n -> (o n)").partition_broadcast(P))
+
+        offsets = held.tile([P, ENTRIES // 16], U16, name="offsets")
+        nc.sync.dma_start(offsets[:], offs)
+        tokens = held.tile([P, TOKENS], BF16, name="tokens")
+        nc.sync.dma_start(tokens[:], table)
+        weights = held.tile([P, EXPERTS, P], BF16, name="weights")
+        nc.sync.dma_start(weights[:], w.rearrange("e k m -> k e m"))
+
+        scaled = held.tile([P, ENTRIES], F32, name="scaled")
+        for e in range(EXPERTS):
+            piece = slice(e * PIECE, (e + 1) * PIECE)
+            picked = tokens[:].indirect(offsets[:, e * PIECE_COLUMNS : (e + 1) * PIECE_COLUMNS])
+            product = banks.tile([P, PIECE], F32, name="product")
+            nc.tensor.matmul(product[:], weights[:, e, :], picked, start=True, stop=True)
+            nc.vector.tensor_tensor(scaled[:, piece], product[:], gains[:, piece], mybir.AluOpType.mult)
+
+        nc.sync.dma_start(out, scaled[:])

@@ -16,24 +16,27 @@ def tile_gather_matmul_kernel(tc, table, w, c, offs, out):
     nc = tc.nc
     with (
         tc.tile_pool(name="held", bufs=1) as held,
+        tc.tile_pool(name="by_expert", bufs=EXPERTS) as by_expert,
         tc.psum_pool(name="banks", bufs=EXPERTS) as banks,
     ):
-        gains = held.tile([P, ENTRIES], F32, name="gains")
-        nc.scalar.dma_start(gains[:], c.rearrange("o n -> (o n)").partition_broadcast(P))
-
         offsets = held.tile([P, ENTRIES // 16], U16, name="offsets")
         nc.sync.dma_start(offsets[:], offs)
         tokens = held.tile([P, TOKENS], BF16, name="tokens")
         nc.sync.dma_start(tokens[:], table)
-        weights = held.tile([P, EXPERTS, P], BF16, name="weights")
-        nc.sync.dma_start(weights[:], w.rearrange("e k m -> k e m"))
 
-        scaled = held.tile([P, ENTRIES], F32, name="scaled")
+        router_row = c.rearrange("o n -> (o n)")
+        weights, gains = [], []
         for e in range(EXPERTS):
-            piece = slice(e * PIECE, (e + 1) * PIECE)
+            weights.append(by_expert.tile([P, P], BF16, name="weights"))
+            nc.sync.dma_start(weights[e][:], w[e])
+            gains.append(by_expert.tile([P, PIECE], F32, name="gains"))
+            nc.scalar.dma_start(gains[e][:], router_row[e * PIECE : (e + 1) * PIECE].partition_broadcast(P))
+
+        for e in range(EXPERTS):
             picked = tokens[:].indirect(offsets[:, e * PIECE_COLUMNS : (e + 1) * PIECE_COLUMNS])
             product = banks.tile([P, PIECE], F32, name="product")
-            nc.tensor.matmul(product[:], weights[:, e, :], picked, start=True, stop=True)
-            nc.vector.tensor_tensor(scaled[:, piece], product[:], gains[:, piece], mybir.AluOpType.mult)
-
-        nc.sync.dma_start(out, scaled[:])
+            nc.tensor.matmul(product[:], weights[e][:], picked, start=True, stop=True)
+            scaled = by_expert.tile([P, PIECE], F32, name="scaled")
+            nc.vector.tensor_tensor(scaled[:], product[:], gains[e][:], mybir.AluOpType.mult)
+            store_queue = nc.sync if e % 2 == 0 else nc.scalar
+            store_queue.dma_start(out[:, e * PIECE : (e + 1) * PIECE], scaled[:])

@@ -23,19 +23,19 @@ def tile_gather_matmul_kernel(tc, table, w, c, offs, out):
         nc.sync.dma_start(offsets[:], offs)
         tokens = held.tile([P, TOKENS], BF16, name="tokens")
         nc.sync.dma_start(tokens[:], table)
+        weights = held.tile([P, EXPERTS, P], BF16, name="weights")
+        nc.sync.dma_start(weights[:], w.rearrange("e k m -> k e m"))
 
         router_row = c.rearrange("o n -> (o n)")
-        weights, gains = [], []
+        gains = []
         for e in range(EXPERTS):
-            weights.append(by_expert.tile([P, P], BF16, name="weights"))
-            nc.sync.dma_start(weights[e][:], w[e])
             gains.append(by_expert.tile([P, PIECE], F32, name="gains"))
             nc.scalar.dma_start(gains[e][:], router_row[e * PIECE : (e + 1) * PIECE].partition_broadcast(P))
 
         for e in range(EXPERTS):
             picked = tokens[:].indirect(offsets[:, e * PIECE_COLUMNS : (e + 1) * PIECE_COLUMNS])
             product = banks.tile([P, PIECE], F32, name="product")
-            nc.tensor.matmul(product[:], weights[e][:], picked, start=True, stop=True)
+            nc.tensor.matmul(product[:], weights[:, e, :], picked, start=True, stop=True)
             scaled = by_expert.tile([P, PIECE], F32, name="scaled")
             nc.vector.tensor_tensor(scaled[:], product[:], gains[e][:], mybir.AluOpType.mult)
             store_queue = nc.sync if e % 2 == 0 else nc.scalar

@@ -16,27 +16,24 @@ def tile_gather_matmul_kernel(tc, table, w, c, offs, out):
     nc = tc.nc
     with (
         tc.tile_pool(name="held", bufs=1) as held,
-        tc.tile_pool(name="by_expert", bufs=EXPERTS) as by_expert,
         tc.psum_pool(name="banks", bufs=EXPERTS) as banks,
     ):
         offsets = held.tile([P, ENTRIES // 16], U16, name="offsets")
         nc.sync.dma_start(offsets[:], offs)
+        weights = held.tile([P, EXPERTS, P], BF16, name="weights")
+        nc.scalar.dma_start(weights[:], w.rearrange("e k m -> k e m"))
         tokens = held.tile([P, TOKENS], BF16, name="tokens")
         nc.sync.dma_start(tokens[:], table)
-        weights = held.tile([P, EXPERTS, P], BF16, name="weights")
-        nc.sync.dma_start(weights[:], w.rearrange("e k m -> k e m"))
 
-        router_row = c.rearrange("o n -> (o n)")
-        gains = []
-        for e in range(EXPERTS):
-            gains.append(by_expert.tile([P, PIECE], F32, name="gains"))
-            nc.scalar.dma_start(gains[e][:], router_row[e * PIECE : (e + 1) * PIECE].partition_broadcast(P))
+        gains = held.tile([P, ENTRIES], F32, name="gains")
+        nc.scalar.dma_start(gains[:], c.rearrange("o n -> (o n)").partition_broadcast(P))
 
+        scaled = held.tile([P, ENTRIES], F32, name="scaled")
         for e in range(EXPERTS):
+            piece = slice(e * PIECE, (e + 1) * PIECE)
             picked = tokens[:].indirect(offsets[:, e * PIECE_COLUMNS : (e + 1) * PIECE_COLUMNS])
             product = banks.tile([P, PIECE], F32, name="product")
             nc.tensor.matmul(product[:], weights[:, e, :], picked, start=True, stop=True)
-            scaled = by_expert.tile([P, PIECE], F32, name="scaled")
-            nc.vector.tensor_tensor(scaled[:], product[:], gains[e][:], mybir.AluOpType.mult)
-            store_queue = nc.sync if e % 2 == 0 else nc.scalar
-            store_queue.dma_start(out[:, e * PIECE : (e + 1) * PIECE], scaled[:])
+            nc.vector.tensor_tensor(scaled[:, piece], product[:], gains[:, piece], mybir.AluOpType.mult)
+
+        nc.sync.dma_start(out, scaled[:])

@@ -8,6 +8,9 @@ EXPERTS = 4
 PIECE = 128
 ENTRIES = EXPERTS * PIECE
 PIECE_COLUMNS = PIECE // 16
+BLOCK = 32
+RUN = ENTRIES // BLOCK
+PIECE_RUNS = PIECE // RUN
 
 FLOPS = 2 * P * P * ENTRIES
 
@@ -20,13 +23,22 @@ def tile_gather_matmul_kernel(tc, table, w, c, offs, out):
     ):
         offsets = held.tile([P, ENTRIES // 16], U16, name="offsets")
         nc.sync.dma_start(offsets[:], offs)
-        weights = held.tile([P, EXPERTS, P], BF16, name="weights")
-        nc.scalar.dma_start(weights[:], w.rearrange("e k m -> k e m"))
+        gain_runs = held.tile([P, RUN], F32, name="gain_runs")
+        nc.scalar.dma_start(
+            gain_runs[:], c.rearrange("o (s b) -> o s b", b=RUN).to_broadcast([P // BLOCK, BLOCK, RUN])
+        )
         tokens = held.tile([P, TOKENS], BF16, name="tokens")
         nc.sync.dma_start(tokens[:], table)
+        weights = held.tile([P, EXPERTS, P], BF16, name="weights")
+        nc.scalar.dma_start(weights[:], w.rearrange("e k m -> k e m"))
 
-        gains = held.tile([P, ENTRIES], F32, name="gains")
-        nc.scalar.dma_start(gains[:], c.rearrange("o n -> (o n)").partition_broadcast(P))
+        repeated = held.tile([P, ENTRIES], F32, name="repeated", align_bytes=64)
+        nc.vector.tensor_copy(
+            repeated[:].rearrange("p (b r) -> p b r", r=BLOCK), gain_runs[:].unsqueeze(2).to_broadcast([P, RUN, BLOCK])
+        )
+        gains = held.tile([P, ENTRIES], F32, name="gains", align_bytes=64)
+        nc.vector.transpose(gains[:], repeated[:])
+        gains_in_order = gains[:].rearrange("m (b s) -> m s b", s=BLOCK)
 
         scaled = held.tile([P, ENTRIES], F32, name="scaled")
         for e in range(EXPERTS):
@@ -34,6 +46,11 @@ def tile_gather_matmul_kernel(tc, table, w, c, offs, out):
             picked = tokens[:].indirect(offsets[:, e * PIECE_COLUMNS : (e + 1) * PIECE_COLUMNS])
             product = banks.tile([P, PIECE], F32, name="product")
             nc.tensor.matmul(product[:], weights[:, e, :], picked, start=True, stop=True)
-            nc.vector.tensor_tensor(scaled[:, piece], product[:], gains[:, piece], mybir.AluOpType.mult)
+            nc.vector.tensor_tensor(
+                scaled[:, piece].rearrange("m (s b) -> m s b", b=RUN),
+                product[:].rearrange("m (s b) -> m s b", b=RUN),
+                gains_in_order[:, e * PIECE_RUNS : (e + 1) * PIECE_RUNS, :],
+                mybir.AluOpType.mult,
+            )
 
         nc.sync.dma_start(out, scaled[:])

@@ -52,5 +52,6 @@ def tile_gather_matmul_kernel(tc, table, w, c, offs, out):
                 gains_in_order[:, e * PIECE_RUNS : (e + 1) * PIECE_RUNS, :],
                 mybir.AluOpType.mult,
             )
-
-        nc.sync.dma_start(out, scaled[:])
+            if e % 2 == 1:
+                half = slice((e - 1) * PIECE, (e + 1) * PIECE)
+                nc.sync.dma_start(out[:, half], scaled[:, half])

@@ -11,6 +11,7 @@ PIECE_COLUMNS = PIECE // 16
 BLOCK = 32
 RUN = ENTRIES // BLOCK
 PIECE_RUNS = PIECE // RUN
+GRID = 256
 
 FLOPS = 2 * P * P * ENTRIES
 
@@ -21,15 +22,15 @@ def tile_gather_matmul_kernel(tc, table, w, c, offs, out):
         tc.tile_pool(name="held", bufs=1) as held,
         tc.psum_pool(name="banks", bufs=EXPERTS) as banks,
     ):
-        offsets = held.tile([P, ENTRIES // 16], U16, name="offsets")
+        offsets = held.tile([P, ENTRIES // 16], U16, name="offsets", align_bytes=GRID)
         nc.sync.dma_start(offsets[:], offs)
-        gain_runs = held.tile([P, RUN], F32, name="gain_runs")
+        gain_runs = held.tile([P, RUN], F32, name="gain_runs", align_bytes=GRID)
         nc.scalar.dma_start(
             gain_runs[:], c.rearrange("o (s b) -> o s b", b=RUN).to_broadcast([P // BLOCK, BLOCK, RUN])
         )
-        tokens = held.tile([P, TOKENS], BF16, name="tokens")
+        tokens = held.tile([P, TOKENS], BF16, name="tokens", align_bytes=GRID)
         nc.sync.dma_start(tokens[:], table)
-        weights = held.tile([P, EXPERTS, P], BF16, name="weights")
+        weights = held.tile([P, EXPERTS, P], BF16, name="weights", align_bytes=GRID)
         nc.scalar.dma_start(weights[:], w.rearrange("e k m -> k e m"))
 
         repeated = held.tile([P, ENTRIES], F32, name="repeated", align_bytes=64)
@@ -40,7 +41,7 @@ def tile_gather_matmul_kernel(tc, table, w, c, offs, out):
         nc.vector.transpose(gains[:], repeated[:])
         gains_in_order = gains[:].rearrange("m (b s) -> m s b", s=BLOCK)
 
-        scaled = held.tile([P, ENTRIES], F32, name="scaled")
+        scaled = held.tile([P, ENTRIES], F32, name="scaled", align_bytes=GRID)
         for e in range(EXPERTS):
             piece = slice(e * PIECE, (e + 1) * PIECE)
             picked = tokens[:].indirect(offsets[:, e * PIECE_COLUMNS : (e + 1) * PIECE_COLUMNS])

@@ -11,6 +11,9 @@ PIECE_COLUMNS = PIECE // 16
 BLOCK = 32
 RUN = ENTRIES // BLOCK
 PIECE_RUNS = PIECE // RUN
+HALF = ENTRIES // 2
+BANK = 512
+WARM_UPS = 4
 GRID = 256
 
 FLOPS = 2 * P * P * ENTRIES
@@ -21,6 +24,7 @@ def tile_gather_matmul_kernel(tc, table, w, c, offs, out):
     with (
         tc.tile_pool(name="held", bufs=1) as held,
         tc.psum_pool(name="banks", bufs=EXPERTS) as banks,
+        tc.psum_pool(name="unused", bufs=1) as unused,
     ):
         offsets = held.tile([P, ENTRIES // 16], U16, name="offsets", align_bytes=GRID)
         nc.sync.dma_start(offsets[:], offs)
@@ -31,14 +35,31 @@ def tile_gather_matmul_kernel(tc, table, w, c, offs, out):
         tokens = held.tile([P, TOKENS], BF16, name="tokens", align_bytes=GRID)
         nc.sync.dma_start(tokens[:], table)
         weights = held.tile([P, EXPERTS, P], BF16, name="weights", align_bytes=GRID)
-        nc.scalar.dma_start(weights[:], w.rearrange("e k m -> k e m"))
+        matrices = w.rearrange("e k m -> k e m")
+        nc.scalar.dma_start(weights[:, 0 : EXPERTS // 2, :], matrices[:, 0 : EXPERTS // 2, :])
+        nc.scalar.dma_start(weights[:, EXPERTS // 2 : EXPERTS, :], matrices[:, EXPERTS // 2 : EXPERTS, :])
+
+        zeros = held.tile([P, P], BF16, name="zeros")
+        nc.vector.memset(zeros[:], 0.0)
+        nothing = unused.tile([P, BANK], F32, name="nothing")
+        for i in range(WARM_UPS):
+            nc.tensor.matmul(
+                nothing[:].rearrange("m (a n) -> m a n", n=P),
+                zeros[:],
+                zeros[:].unsqueeze(1).to_broadcast([P, BANK // P, P]),
+                start=True,
+                stop=True,
+            )
 
         repeated = held.tile([P, ENTRIES], F32, name="repeated", align_bytes=64)
-        nc.vector.tensor_copy(
-            repeated[:].rearrange("p (b r) -> p b r", r=BLOCK), gain_runs[:].unsqueeze(2).to_broadcast([P, RUN, BLOCK])
-        )
         gains = held.tile([P, ENTRIES], F32, name="gains", align_bytes=64)
-        nc.vector.transpose(gains[:], repeated[:])
+        for h in range(2):
+            nc.vector.tensor_copy(
+                repeated[:, h * HALF : (h + 1) * HALF].rearrange("p (b r) -> p b r", r=BLOCK),
+                gain_runs[:, h * (RUN // 2) : (h + 1) * (RUN // 2)].unsqueeze(2).to_broadcast([P, RUN // 2, BLOCK]),
+            )
+        for h in range(2):
+            nc.vector.transpose(gains[:, h * HALF : (h + 1) * HALF], repeated[:, h * HALF : (h + 1) * HALF])
         gains_in_order = gains[:].rearrange("m (b s) -> m s b", s=BLOCK)
 
         scaled = held.tile([P, ENTRIES], F32, name="scaled", align_bytes=GRID)

@@ -9,9 +9,9 @@ PIECE = 128
 ENTRIES = EXPERTS * PIECE
 PIECE_COLUMNS = PIECE // 16
 BLOCK = 32
-RUN = ENTRIES // BLOCK
-PIECE_RUNS = PIECE // RUN
+RUNS = ENTRIES // BLOCK
 HALF = ENTRIES // 2
+HALF_RUNS = RUNS // 2
 BANK = 512
 WARM_UPS = 4
 GRID = 256
@@ -28,9 +28,9 @@ def tile_gather_matmul_kernel(tc, table, w, c, offs, out):
     ):
         offsets = held.tile([P, ENTRIES // 16], U16, name="offsets", align_bytes=GRID)
         nc.sync.dma_start(offsets[:], offs)
-        gain_runs = held.tile([P, RUN], F32, name="gain_runs", align_bytes=GRID)
+        gain_runs = held.tile([P, BLOCK], F32, name="gain_runs", align_bytes=GRID)
         nc.scalar.dma_start(
-            gain_runs[:], c.rearrange("o (s b) -> o s b", b=RUN).to_broadcast([P // BLOCK, BLOCK, RUN])
+            gain_runs[:], c.rearrange("o (s b) -> o s b", b=BLOCK).to_broadcast([P // RUNS, RUNS, BLOCK])
         )
         tokens = held.tile([P, TOKENS], BF16, name="tokens", align_bytes=GRID)
         nc.sync.dma_start(tokens[:], table)
@@ -51,16 +51,17 @@ def tile_gather_matmul_kernel(tc, table, w, c, offs, out):
                 stop=True,
             )
 
+        turned = held.tile([P, BLOCK], F32, name="turned", align_bytes=64)
+        nc.vector.transpose(turned[:], gain_runs[:])
         repeated = held.tile([P, ENTRIES], F32, name="repeated", align_bytes=64)
         gains = held.tile([P, ENTRIES], F32, name="gains", align_bytes=64)
         for h in range(2):
             nc.vector.tensor_copy(
-                repeated[:, h * HALF : (h + 1) * HALF].rearrange("p (b r) -> p b r", r=BLOCK),
-                gain_runs[:, h * (RUN // 2) : (h + 1) * (RUN // 2)].unsqueeze(2).to_broadcast([P, RUN // 2, BLOCK]),
+                repeated[:, h * HALF : (h + 1) * HALF].rearrange("p (s r) -> p s r", r=BLOCK),
+                turned[:, h * HALF_RUNS : (h + 1) * HALF_RUNS].unsqueeze(2).to_broadcast([P, HALF_RUNS, BLOCK]),
             )
         for h in range(2):
             nc.vector.transpose(gains[:, h * HALF : (h + 1) * HALF], repeated[:, h * HALF : (h + 1) * HALF])
-        gains_in_order = gains[:].rearrange("m (b s) -> m s b", s=BLOCK)
 
         scaled = held.tile([P, ENTRIES], F32, name="scaled", align_bytes=GRID)
         for e in range(EXPERTS):
@@ -68,12 +69,7 @@ def tile_gather_matmul_kernel(tc, table, w, c, offs, out):
             picked = tokens[:].indirect(offsets[:, e * PIECE_COLUMNS : (e + 1) * PIECE_COLUMNS])
             product = banks.tile([P, PIECE], F32, name="product")
             nc.tensor.matmul(product[:], weights[:, e, :], picked, start=True, stop=True)
-            nc.vector.tensor_tensor(
-                scaled[:, piece].rearrange("m (s b) -> m s b", b=RUN),
-                product[:].rearrange("m (s b) -> m s b", b=RUN),
-                gains_in_order[:, e * PIECE_RUNS : (e + 1) * PIECE_RUNS, :],
-                mybir.AluOpType.mult,
-            )
+            nc.vector.tensor_tensor(scaled[:, piece], product[:], gains[:, piece], mybir.AluOpType.mult)
             if e % 2 == 1:
                 half = slice((e - 1) * PIECE, (e + 1) * PIECE)
                 nc.sync.dma_start(out[:, half], scaled[:, half])

@@ -12,8 +12,6 @@ BLOCK = 32
 RUNS = ENTRIES // BLOCK
 HALF = ENTRIES // 2
 HALF_RUNS = RUNS // 2
-BANK = 512
-WARM_UPS = 4
 GRID = 256
 
 FLOPS = 2 * P * P * ENTRIES
@@ -24,7 +22,6 @@ def tile_gather_matmul_kernel(tc, table, w, c, offs, out):
     with (
         tc.tile_pool(name="held", bufs=1) as held,
         tc.psum_pool(name="banks", bufs=EXPERTS) as banks,
-        tc.psum_pool(name="unused", bufs=1) as unused,
     ):
         offsets = held.tile([P, ENTRIES // 16], U16, name="offsets", align_bytes=GRID)
         nc.sync.dma_start(offsets[:], offs)
@@ -38,18 +35,6 @@ def tile_gather_matmul_kernel(tc, table, w, c, offs, out):
         matrices = w.rearrange("e k m -> k e m")
         nc.scalar.dma_start(weights[:, 0 : EXPERTS // 2, :], matrices[:, 0 : EXPERTS // 2, :])
         nc.scalar.dma_start(weights[:, EXPERTS // 2 : EXPERTS, :], matrices[:, EXPERTS // 2 : EXPERTS, :])
-
-        zeros = held.tile([P, P], BF16, name="zeros")
-        nc.vector.memset(zeros[:], 0.0)
-        nothing = unused.tile([P, BANK], F32, name="nothing")
-        for i in range(WARM_UPS):
-            nc.tensor.matmul(
-                nothing[:].rearrange("m (a n) -> m a n", n=P),
-                zeros[:],
-                zeros[:].unsqueeze(1).to_broadcast([P, BANK // P, P]),
-                start=True,
-                stop=True,
-            )
 
         turned = held.tile([P, BLOCK], F32, name="turned", align_bytes=64)
         nc.vector.transpose(turned[:], gain_runs[:])

@@ -32,9 +32,7 @@ def tile_gather_matmul_kernel(tc, table, w, c, offs, out):
         tokens = held.tile([P, TOKENS], BF16, name="tokens", align_bytes=GRID)
         nc.sync.dma_start(tokens[:], table)
         weights = held.tile([P, EXPERTS, P], BF16, name="weights", align_bytes=GRID)
-        matrices = w.rearrange("e k m -> k e m")
-        nc.scalar.dma_start(weights[:, 0 : EXPERTS // 2, :], matrices[:, 0 : EXPERTS // 2, :])
-        nc.scalar.dma_start(weights[:, EXPERTS // 2 : EXPERTS, :], matrices[:, EXPERTS // 2 : EXPERTS, :])
+        nc.scalar.dma_start(weights[:], w.rearrange("e k m -> k e m"))
 
         turned = held.tile([P, BLOCK], F32, name="turned", align_bytes=64)
         nc.vector.transpose(turned[:], gain_runs[:])

import concourse.mybir as mybir

BF16, F32, U16 = mybir.dt.bfloat16, mybir.dt.float32, mybir.dt.uint16

P = 128
TOKENS = 256
EXPERTS = 4
PIECE = 128
ENTRIES = EXPERTS * PIECE
PIECE_COLUMNS = PIECE // 16
BLOCK = 32
RUNS = ENTRIES // BLOCK
HALF = ENTRIES // 2
HALF_RUNS = RUNS // 2
GRID = 256

FLOPS = 2 * P * P * ENTRIES


def tile_gather_matmul_kernel(tc, table, w, c, offs, out):
    nc = tc.nc
    with (
        tc.tile_pool(name="held", bufs=1) as held,
        tc.psum_pool(name="banks", bufs=EXPERTS) as banks,
    ):
        offsets = held.tile([P, ENTRIES // 16], U16, name="offsets", align_bytes=GRID)
        nc.sync.dma_start(offsets[:], offs)
        gain_runs = held.tile([P, BLOCK], F32, name="gain_runs", align_bytes=GRID)
        nc.scalar.dma_start(
            gain_runs[:], c.rearrange("o (s b) -> o s b", b=BLOCK).to_broadcast([P // RUNS, RUNS, BLOCK])
        )
        tokens = held.tile([P, TOKENS], BF16, name="tokens", align_bytes=GRID)
        nc.sync.dma_start(tokens[:], table)
        weights = held.tile([P, EXPERTS, P], BF16, name="weights", align_bytes=GRID)
        nc.scalar.dma_start(weights[:], w.rearrange("e k m -> k e m"))

        turned = held.tile([P, BLOCK], F32, name="turned", align_bytes=64)
        nc.vector.transpose(turned[:], gain_runs[:])
        repeated = held.tile([P, ENTRIES], F32, name="repeated", align_bytes=64)
        gains = held.tile([P, ENTRIES], F32, name="gains", align_bytes=64)
        for h in range(2):
            nc.vector.tensor_copy(
                repeated[:, h * HALF : (h + 1) * HALF].rearrange("p (s r) -> p s r", r=BLOCK),
                turned[:, h * HALF_RUNS : (h + 1) * HALF_RUNS].unsqueeze(2).to_broadcast([P, HALF_RUNS, BLOCK]),
            )
        for h in range(2):
            nc.vector.transpose(gains[:, h * HALF : (h + 1) * HALF], repeated[:, h * HALF : (h + 1) * HALF])

        scaled = held.tile([P, ENTRIES], F32, name="scaled", align_bytes=GRID)
        for e in range(EXPERTS):
            piece = slice(e * PIECE, (e + 1) * PIECE)
            picked = tokens[:].indirect(offsets[:, e * PIECE_COLUMNS : (e + 1) * PIECE_COLUMNS])
            product = banks.tile([P, PIECE], F32, name="product")
            nc.tensor.matmul(product[:], weights[:, e, :], picked, start=True, stop=True)
            nc.vector.tensor_tensor(scaled[:, piece], product[:], gains[:, piece], mybir.AluOpType.mult)
            if e % 2 == 1:
                half = slice((e - 1) * PIECE, (e + 1) * PIECE)
                nc.sync.dma_start(out[:, half], scaled[:, half])
